import numpy as np
import ml_dtypes

BF16 = ml_dtypes.bfloat16


def bf(x):
    return np.asarray(x, np.float32).astype(BF16)


def f32(x):
    return np.asarray(x, np.float32)


def f64(x):
    return np.asarray(x).astype(np.float64)


def striped(idx):
    return np.tile(idx.reshape(-1, 16).T, (8, 1))


S, K, M, N, D, V = 2048, 128, 128, 4096, 8, 512


def setup_inputs():
    return {"table": bf(np.random.standard_normal((K, S))), "w": bf(np.random.standard_normal((K, M)) / np.sqrt(D * K)), "b": f32(0.5 * np.random.standard_normal((M, 1))), "offs": striped(np.random.permutation(np.tile(np.arange(S), 2))[:N])}


def reference(table, w, b, offs):
    idx = offs[:16].T.reshape(-1)
    x = f64(table)[:, idx]
    y = f64(w).T @ sum(x[:, t * V : (t + 1) * V] for t in range(D))
    return np.tanh(y + f64(b))

@@ -1,0 +1,51 @@
+import concourse.mybir as mybir
+
+BF16, F32, U16 = mybir.dt.bfloat16, mybir.dt.float32, mybir.dt.uint16
+TANH = mybir.ActivationFunctionType.Tanh
+
+FEATURES = 128
+OUT_FEATURES = 128
+TABLE_NODES = 2048
+NEIGHBOURS = 8
+OUT_NODES = 512
+ENTRIES_PER_COLUMN = 16
+LIST_COLUMNS = NEIGHBOURS * OUT_NODES // ENTRIES_PER_COLUMN
+PIECE_COLUMNS = OUT_NODES // ENTRIES_PER_COLUMN
+
+FLOPS = 2 * FEATURES * OUT_FEATURES * OUT_NODES * NEIGHBOURS
+
+
+def tile_gather_matmul_kernel(tc, table, w, b, offs, out):
+    nc = tc.nc
+    with (
+        tc.tile_pool(name="held", bufs=1) as held,
+        tc.psum_pool(name="psum", bufs=1) as psum,
+    ):
+        table_tile = held.tile([FEATURES, TABLE_NODES], BF16, name="table_tile")
+        offsets = held.tile([128, LIST_COLUMNS], U16, name="offsets")
+        weights = held.tile([FEATURES, OUT_FEATURES], BF16, name="weights")
+        bias = held.tile([OUT_FEATURES, 1], F32, name="bias")
+        result = held.tile([OUT_FEATURES, OUT_NODES], F32, name="result")
+        warm = held.tile([128, 1], F32, name="warm")
+        summed = psum.tile([OUT_FEATURES, OUT_NODES], F32, name="summed")
+
+        nc.sync.dma_start(table_tile[:], table)
+        nc.sync.dma_start(offsets[:], offs)
+        nc.sync.dma_start(weights[:], w)
+        nc.scalar.dma_start(bias[:], b)
+
+        nc.vector.memset(warm[:], 0.0)
+        nc.scalar.activation(warm[:], warm[:], TANH)
+
+        for t in range(NEIGHBOURS):
+            piece = offsets[:, t * PIECE_COLUMNS : (t + 1) * PIECE_COLUMNS]
+            nc.tensor.matmul(
+                summed[:],
+                weights[:],
+                table_tile[:].indirect(piece),
+                start=(t == 0),
+                stop=(t == NEIGHBOURS - 1),
+            )
+
+        nc.scalar.activation(result[:], summed[:], TANH, bias=bias[:])
+        nc.sync.dma_start(out, result[:])

@@ -10,7 +10,8 @@ NEIGHBOURS = 8
 OUT_NODES = 512
 ENTRIES_PER_COLUMN = 16
 LIST_COLUMNS = NEIGHBOURS * OUT_NODES // ENTRIES_PER_COLUMN
-PIECE_COLUMNS = OUT_NODES // ENTRIES_PER_COLUMN
+HALF = OUT_NODES // 2
+HALF_COLUMNS = HALF // ENTRIES_PER_COLUMN
 
 FLOPS = 2 * FEATURES * OUT_FEATURES * OUT_NODES * NEIGHBOURS
 
@@ -25,9 +26,7 @@ def tile_gather_matmul_kernel(tc, table, w, b, offs, out):
         offsets = held.tile([128, LIST_COLUMNS], U16, name="offsets")
         weights = held.tile([FEATURES, OUT_FEATURES], BF16, name="weights")
         bias = held.tile([OUT_FEATURES, 1], F32, name="bias")
-        result = held.tile([OUT_FEATURES, OUT_NODES], F32, name="result")
         warm = held.tile([128, 1], F32, name="warm")
-        summed = psum.tile([OUT_FEATURES, OUT_NODES], F32, name="summed")
 
         nc.sync.dma_start(table_tile[:], table)
         nc.sync.dma_start(offsets[:], offs)
@@ -37,15 +36,19 @@ def tile_gather_matmul_kernel(tc, table, w, b, offs, out):
         nc.vector.memset(warm[:], 0.0)
         nc.scalar.activation(warm[:], warm[:], TANH)
 
-        for t in range(NEIGHBOURS):
-            piece = offsets[:, t * PIECE_COLUMNS : (t + 1) * PIECE_COLUMNS]
-            nc.tensor.matmul(
-                summed[:],
-                weights[:],
-                table_tile[:].indirect(piece),
-                start=(t == 0),
-                stop=(t == NEIGHBOURS - 1),
-            )
+        for half, store_queue in enumerate((nc.sync, nc.scalar)):
+            summed = psum.tile([OUT_FEATURES, HALF], F32, name=f"summed_{half}")
+            result = held.tile([OUT_FEATURES, HALF], F32, name=f"result_{half}")
 
-        nc.scalar.activation(result[:], summed[:], TANH, bias=bias[:])
-        nc.sync.dma_start(out, result[:])
+            for t in range(NEIGHBOURS):
+                first = (2 * t + half) * HALF_COLUMNS
+                nc.tensor.matmul(
+                    summed[:],
+                    weights[:],
+                    table_tile[:].indirect(offsets[:, first : first + HALF_COLUMNS]),
+                    start=(t == 0),
+                    stop=(t == NEIGHBOURS - 1),
+                )
+
+            nc.scalar.activation(result[:], summed[:], TANH, bias=bias[:])
+            store_queue.dma_start(out[:, half * HALF : (half + 1) * HALF], result[:])

@@ -28,10 +28,10 @@ def tile_gather_matmul_kernel(tc, table, w, b, offs, out):
         bias = held.tile([OUT_FEATURES, 1], F32, name="bias")
         warm = held.tile([128, 1], F32, name="warm")
 
-        nc.sync.dma_start(table_tile[:], table)
+        nc.scalar.dma_start(table_tile[:], table)
         nc.sync.dma_start(offsets[:], offs)
         nc.sync.dma_start(weights[:], w)
-        nc.scalar.dma_start(bias[:], b)
+        nc.sync.dma_start(bias[:], b)
 
         nc.vector.memset(warm[:], 0.0)
         nc.scalar.activation(warm[:], warm[:], TANH)

import concourse.mybir as mybir

BF16, F32, U16 = mybir.dt.bfloat16, mybir.dt.float32, mybir.dt.uint16
TANH = mybir.ActivationFunctionType.Tanh

FEATURES = 128
OUT_FEATURES = 128
TABLE_NODES = 2048
NEIGHBOURS = 8
OUT_NODES = 512
ENTRIES_PER_COLUMN = 16
LIST_COLUMNS = NEIGHBOURS * OUT_NODES // ENTRIES_PER_COLUMN
HALF = OUT_NODES // 2
HALF_COLUMNS = HALF // ENTRIES_PER_COLUMN

FLOPS = 2 * FEATURES * OUT_FEATURES * OUT_NODES * NEIGHBOURS


def tile_gather_matmul_kernel(tc, table, w, b, offs, out):
    nc = tc.nc
    with (
        tc.tile_pool(name="held", bufs=1) as held,
        tc.psum_pool(name="psum", bufs=1) as psum,
    ):
        table_tile = held.tile([FEATURES, TABLE_NODES], BF16, name="table_tile")
        offsets = held.tile([128, LIST_COLUMNS], U16, name="offsets")
        weights = held.tile([FEATURES, OUT_FEATURES], BF16, name="weights")
        bias = held.tile([OUT_FEATURES, 1], F32, name="bias")
        warm = held.tile([128, 1], F32, name="warm")

        nc.scalar.dma_start(table_tile[:], table)
        nc.sync.dma_start(offsets[:], offs)
        nc.sync.dma_start(weights[:], w)
        nc.sync.dma_start(bias[:], b)

        nc.vector.memset(warm[:], 0.0)
        nc.scalar.activation(warm[:], warm[:], TANH)

        for half, store_queue in enumerate((nc.sync, nc.scalar)):
            summed = psum.tile([OUT_FEATURES, HALF], F32, name=f"summed_{half}")
            result = held.tile([OUT_FEATURES, HALF], F32, name=f"result_{half}")

            for t in range(NEIGHBOURS):
                first = (2 * t + half) * HALF_COLUMNS
                nc.tensor.matmul(
                    summed[:],
                    weights[:],
                    table_tile[:].indirect(offsets[:, first : first + HALF_COLUMNS]),
                    start=(t == 0),
                    stop=(t == NEIGHBOURS - 1),
                )

            nc.scalar.activation(result[:], summed[:], TANH, bias=bias[:])
            store_queue.dma_start(out[:, half * HALF : (half + 1) * HALF], result[:])
